import numpy as np
import ml_dtypes


def mxq(x, axis, fmt="e4m3"):
    dtype, down = {"e4m3": (ml_dtypes.float8_e4m3fn, 7), "e5m2": (ml_dtypes.float8_e5m2, 14)}[fmt]
    v = np.moveaxis(np.asarray(x, np.float32).astype(ml_dtypes.bfloat16).astype(np.float64), axis, -1)
    blocks = v.reshape(v.shape[:-1] + (-1, 32))
    amax = np.abs(blocks).max(-1, keepdims=True)
    byte = np.maximum(np.where(amax > 0, np.frexp(amax)[1] - 1 + 127, 0) - down, 1)
    scale = np.exp2(byte - 127.0)
    codes = (blocks / scale).astype(np.float32).astype(dtype).astype(np.float64)
    return np.moveaxis((codes * scale).reshape(v.shape), -1, axis)


WIDE = False


def mx_kscale(k, group=512):
    if not WIDE:
        return np.ones(k)
    levels = np.array([18, -18])
    if group != 512:
        return np.exp2(np.random.permutation(np.resize(levels, k // group))).repeat(group)
    if k % 512:
        return np.exp2(np.random.permutation(np.resize(levels, k // 32))).repeat(32)
    a = np.empty((k // 512, 16))
    for p in range(k // 512):
        a[p, :8] = np.random.permutation(np.resize(levels, 8))
        for g in range(8):
            far = levels[np.abs(levels - a[p, g]) >= 10]
            a[p, g + 8] = far[np.random.randint(len(far))]
    return np.exp2(a.ravel()).repeat(32)


def f64(x):
    return np.asarray(x).astype(np.float64)


G, D, M, N = 4, 128, 128, 512


def setup_inputs():
    n = np.random.standard_normal
    s_d = mx_kscale(D, 0)
    return {
        "x": (n((G, D, N)) * s_d[:, None]).astype(np.float32),
        "w1": (n((G, D, M)) / np.sqrt(D) / s_d[:, None]).astype(np.float32),
        "w2": (n((G, D, M)) / np.sqrt(D) / s_d[:, None]).astype(np.float32),
        "tp": (np.random.uniform(0.5, 1.2, (G, M, 1))).astype(np.float32),
        "dx": (n((G, D, N)) * s_d[:, None]).astype(np.float32),
        "og": (np.random.uniform(0.5, 2.0, (G, M, 1))).astype(np.float32),
        "base": (0.3 * n((G, M, N))).astype(np.float32),
    }


def reference(x, w1, w2, tp, dx, og, base):
    w1q = mxq(f64(w1), 1, "e4m3")
    xq = mxq(f64(x), 1, "e4m3")
    z1 = w1q.transpose(0, 2, 1) @ xq
    dxq = mxq(f64(dx), 1, "e4m3")
    tz1 = w1q.transpose(0, 2, 1) @ dxq
    w2q = mxq(f64(w2), 1, "e4m3")
    z2 = w2q.transpose(0, 2, 1) @ xq
    tz2 = w2q.transpose(0, 2, 1) @ dxq
    p1 = np.exp(z1 * f64(tp) - np.max(z1 * f64(tp), axis=-1, keepdims=True))
    zs = np.sum(p1, axis=-1, keepdims=True)
    xp1 = tz1 * f64(tp) * p1
    xzs = np.sum(xp1, axis=-1, keepdims=True)
    xh = ((xp1 - xzs * p1 / zs) / zs * z2 + tz2 * p1 / zs) * 512.0
    y = xh * f64(og) + f64(base)
    return y

@@ -1,0 +1,228 @@
+from contextlib import ExitStack
+
+import concourse.mybir as mybir
+
+G, D, M, N = 4, 128, 128, 512
+FLOPS = 4 * 2 * G * D * M * N
+
+F32 = mybir.dt.float32
+BF16 = mybir.dt.bfloat16
+U32 = mybir.dt.uint32
+U8 = mybir.dt.uint8
+FP8X4 = mybir.dt.float8_e4m3fn_x4
+ALU = mybir.AluOpType
+ACT = mybir.ActivationFunctionType
+
+P = 128
+PACK = 4
+ROWS = D // PACK
+X_SPLIT = 336
+DX_SPLIT = 288
+
+
+def tile_rows_tnrowsoft_kernel(tc, x, w1, w2, tp, dx, og, base, out):
+    nc = tc.nc
+    with ExitStack() as ctx:
+        sb = ctx.enter_context(tc.tile_pool(name="sb", bufs=1))
+        ps = ctx.enter_context(tc.psum_pool(name="ps", bufs=1))
+        ctx.enter_context(tc.manual_schedule())
+
+        def load(name, src, width):
+            raw = sb.tile([P, PACK * width], F32, name=name + "_raw", align_bytes=64)
+            nc.sync.dma_start(out=raw[:], in_=src.rearrange("g (p j) n -> (g p) (j n)", j=PACK))
+            return raw
+
+        def mx_tiles(name, width):
+            words = sb.tile([P, PACK * width], BF16, name=name + "_bf", align_bytes=64)
+            codes = sb.tile([P, width], U32, name=name + "_codes", align_bytes=64)
+            scales = sb.tile([P, width], U8, name=name + "_scales", align_bytes=64)
+            return words, codes, scales
+
+        def views(raw, words, lo, hi):
+            src = raw[:].rearrange("p (j c i) -> p c j i", j=PACK, i=4)[:, lo // 4 : hi // 4, :, :]
+            dst = words[:].rearrange("p (c i j) -> p c j i", i=4, j=PACK)[:, lo // 4 : hi // 4, :, :]
+            return src, dst
+
+        def inter_vector(raw, op, lo, hi):
+            src, dst = views(raw, op[0], lo, hi)
+            nc.vector.tensor_copy(out=dst, in_=src)
+
+        def inter_scalar(raw, op, lo, hi):
+            src, dst = views(raw, op[0], lo, hi)
+            nc.scalar.copy(out=dst, in_=src)
+
+        def inter_gpsimd(raw, op, lo, hi):
+            src = raw[:].rearrange("p (j n) -> p n j", j=PACK)[:, lo:hi, :]
+            dst = op[0][:].rearrange("p (n j) -> p n j", j=PACK)[:, lo:hi, :]
+            nc.gpsimd.tensor_scalar(out=dst, in0=src, scalar1=1.0, scalar2=0.0, op0=ALU.mult, op1=ALU.add)
+
+        def quantize(op):
+            nc.vector.quantize_mx(out=op[1][:].bitcast(FP8X4), scales=op[2][:], in_=op[0][:])
+
+        def product(bank, w, v, g):
+            rows = slice(ROWS * g, ROWS * (g + 1))
+            nc.tensor.matmul_mx(
+                out=bank[:],
+                lhsT=w[1][rows, :].bitcast(FP8X4),
+                lhsT_scale=w[2][rows, :],
+                rhs=v[1][rows, :].bitcast(FP8X4),
+                rhs_scale=v[2][rows, :],
+                start=True,
+                stop=True,
+            )
+
+        def big(name):
+            return [sb.tile([P, N], F32, name=name + str(g)) for g in range(G)]
+
+        bank_a = [ps.tile([P, N], F32, name="bank_a" + str(g)) for g in range(G)]
+        bank_b = [ps.tile([P, N], F32, name="bank_b" + str(g)) for g in range(G)]
+
+        rows_in = sb.tile([P, P], F32, name="rows_in", align_bytes=64)
+        cols = sb.tile([P, P], F32, name="cols", align_bytes=64)
+        warm = sb.tile([P, 1], F32, name="warm")
+        zero = sb.tile([P, 1], F32, name="zero")
+        nc.vector.memset(rows_in[:], 0.0)
+        nc.vector.memset(zero[:], 0.0)
+
+        w1_raw = load("w1", w1, M)
+        x_raw = load("x", x, N)
+        for r, vec in enumerate((tp, og)):
+            nc.sync.dma_start(
+                out=rows_in[r:P:32, :].rearrange("q (g j) -> q g j", g=G),
+                in_=vec.rearrange("g (q j) o -> q g (j o)", j=32),
+            )
+        w2_raw = load("w2", w2, M)
+        dx_raw = load("dx", dx, N)
+        base_sb = sb.tile([P, G * N], F32, name="base_sb")
+        nc.sync.dma_start(out=base_sb[:].rearrange("m (g n) -> m g n", g=G), in_=base.rearrange("g m n -> m g n"))
+        nc.scalar.activation(out=warm[:], in_=zero[:], func=ACT.Exp)
+
+        w1q = mx_tiles("w1", M)
+        w2q = mx_tiles("w2", M)
+        xq = mx_tiles("x", N)
+        dxq = mx_tiles("dx", N)
+
+        neg_tp = sb.tile([P, G], F32, name="neg_tp")
+        gain = sb.tile([P, 2 * G], F32, name="gain")
+        neg_max = sb.tile([P, G], F32, name="neg_max")
+        zsum = sb.tile([P, G], F32, name="zsum")
+        inv = sb.tile([P, G], F32, name="inv")
+        mean = sb.tile([P, G], F32, name="mean")
+        fac = sb.tile([P, 2 * G], F32, name="fac")
+        neg_s, prob, z2s, part, dsum, scaled, res = (big(n) for n in ("neg_s", "prob", "z2s", "part", "dsum", "scaled", "res"))
+
+        inter_vector(w1_raw, w1q, 0, M)
+        quantize(w1q)
+
+        inter_vector(x_raw, xq, 0, X_SPLIT)
+        inter_scalar(x_raw, xq, X_SPLIT, N)
+        quantize(xq)
+        for g in range(G):
+            product(bank_a[g], w1q, xq, g)
+        inter_scalar(w2_raw, w2q, 0, M)
+        nc.vector.transpose(out=cols[:], in_=rows_in[:])
+        quantize(w2q)
+        for g in range(G):
+            product(bank_b[g], w2q, xq, g)
+        tp_cols = cols[:, 0:P:32]
+        og_cols = cols[:, 1:P:32]
+        nc.vector.tensor_scalar(out=neg_tp[:], in0=tp_cols, scalar1=-1.0, scalar2=None, op0=ALU.mult)
+        nc.vector.tensor_scalar(out=gain[:, 0 : 2 * G : 2], in0=og_cols, scalar1=float(N), scalar2=None, op0=ALU.mult)
+        nc.vector.scalar_tensor_tensor(
+            out=gain[:, 1 : 2 * G : 2], in0=og_cols, scalar=float(N), in1=tp_cols, op0=ALU.mult, op1=ALU.mult
+        )
+
+        inter_gpsimd(dx_raw, dxq, 0, DX_SPLIT)
+        inter_scalar(dx_raw, dxq, DX_SPLIT, N)
+
+        def row_max(g):
+            nc.vector.tensor_scalar(
+                out=neg_s[g][:], in0=bank_a[g][:], scalar1=neg_tp[:, g : g + 1], scalar2=None,
+                op0=ALU.mult, op1=ALU.min, accum_out=neg_max[:, g : g + 1],
+            )
+
+        def exp(g):
+            nc.scalar.activation(
+                out=prob[g][:], in_=neg_s[g][:], func=ACT.Exp, scale=-1.0,
+                bias=neg_max[:, g : g + 1], accum_out=zsum[:, g : g + 1],
+            )
+
+        def recip(g0):
+            nc.vector.reciprocal(out=inv[:, g0 : g0 + 2], in_=zsum[:, g0 : g0 + 2])
+
+        def factors(g):
+            nc.scalar.activation(
+                out=fac[:, 2 * g : 2 * g + 2], in_=gain[:, 2 * g : 2 * g + 2], func=ACT.Copy, scale=inv[:, g : g + 1]
+            )
+
+        def scale_z2(g):
+            nc.scalar.activation(out=z2s[g][:], in_=bank_b[g][:], func=ACT.Copy, scale=fac[:, 2 * g + 1 : 2 * g + 2])
+            product(bank_b[g], w2q, dxq, g)
+
+        def mean_tz1(g):
+            nc.vector.scalar_tensor_tensor(
+                out=part[g][:], in0=bank_a[g][:], scalar=inv[:, g : g + 1], in1=prob[g][:],
+                op0=ALU.mult, op1=ALU.mult, accum_out=mean[:, g : g + 1],
+            )
+
+        def centred(g):
+            nc.vector.scalar_tensor_tensor(
+                out=part[g][:], in0=bank_a[g][:], scalar=mean[:, g : g + 1], in1=z2s[g][:],
+                op0=ALU.subtract, op1=ALU.mult,
+            )
+
+        def add_tz2(g):
+            nc.vector.scalar_tensor_tensor(
+                out=dsum[g][:], in0=bank_b[g][:], scalar=fac[:, 2 * g : 2 * g + 1], in1=part[g][:],
+                op0=ALU.mult, op1=ALU.add,
+            )
+
+        def weigh(eng, g):
+            eng.tensor_tensor(out=scaled[g][:], in0=dsum[g][:], in1=prob[g][:], op=ALU.mult)
+
+        def finish(eng, g):
+            eng.tensor_tensor(out=res[g][:], in0=scaled[g][:], in1=base_sb[:, g * N : (g + 1) * N], op=ALU.add)
+            nc.sync.dma_start(out=out[g], in_=res[g][:])
+
+        row_max(0)
+        exp(0)
+        row_max(1)
+        exp(1)
+        row_max(2)
+        exp(2)
+        quantize(dxq)
+        for g in range(3):
+            product(bank_a[g], w1q, dxq, g)
+        recip(0)
+        row_max(3)
+        product(bank_a[3], w1q, dxq, 3)
+        factors(0)
+        factors(1)
+        scale_z2(0)
+        scale_z2(1)
+        exp(3)
+        mean_tz1(0)
+        mean_tz1(1)
+        centred(0)
+        recip(2)
+        factors(2)
+        factors(3)
+        scale_z2(2)
+        scale_z2(3)
+        add_tz2(0)
+        weigh(nc.gpsimd, 0)
+        finish(nc.gpsimd, 0)
+        centred(1)
+        mean_tz1(2)
+        add_tz2(1)
+        weigh(nc.gpsimd, 1)
+        finish(nc.gpsimd, 1)
+        mean_tz1(3)
+        centred(2)
+        centred(3)
+        add_tz2(2)
+        add_tz2(3)
+        weigh(nc.vector, 2)
+        weigh(nc.vector, 3)
+        finish(nc.vector, 2)
+        finish(nc.vector, 3)

@@ -17,7 +17,7 @@ P = 128
 PACK = 4
 ROWS = D // PACK
 X_SPLIT = 336
-DX_SPLIT = 288
+DX_SPLIT = 240
 
 
 def tile_rows_tnrowsoft_kernel(tc, x, w1, w2, tp, dx, og, base, out):
@@ -38,17 +38,17 @@ def tile_rows_tnrowsoft_kernel(tc, x, w1, w2, tp, dx, og, base, out):
             scales = sb.tile([P, width], U8, name=name + "_scales", align_bytes=64)
             return words, codes, scales
 
-        def views(raw, words, lo, hi):
+        def views(raw, words, at, lo, hi):
             src = raw[:].rearrange("p (j c i) -> p c j i", j=PACK, i=4)[:, lo // 4 : hi // 4, :, :]
-            dst = words[:].rearrange("p (c i j) -> p c j i", i=4, j=PACK)[:, lo // 4 : hi // 4, :, :]
+            dst = words[:].rearrange("p (c i j) -> p c j i", i=4, j=PACK)[:, (at + lo) // 4 : (at + hi) // 4, :, :]
             return src, dst
 
-        def inter_vector(raw, op, lo, hi):
-            src, dst = views(raw, op[0], lo, hi)
+        def inter_vector(raw, op, at, lo, hi):
+            src, dst = views(raw, op[0], at, lo, hi)
             nc.vector.tensor_copy(out=dst, in_=src)
 
-        def inter_scalar(raw, op, lo, hi):
-            src, dst = views(raw, op[0], lo, hi)
+        def inter_scalar(raw, op, at, lo, hi):
+            src, dst = views(raw, op[0], at, lo, hi)
             nc.scalar.copy(out=dst, in_=src)
 
         def inter_gpsimd(raw, op, lo, hi):
@@ -56,8 +56,10 @@ def tile_rows_tnrowsoft_kernel(tc, x, w1, w2, tp, dx, og, base, out):
             dst = op[0][:].rearrange("p (n j) -> p n j", j=PACK)[:, lo:hi, :]
             nc.gpsimd.tensor_scalar(out=dst, in0=src, scalar1=1.0, scalar2=0.0, op0=ALU.mult, op1=ALU.add)
 
-        def quantize(op):
-            nc.vector.quantize_mx(out=op[1][:].bitcast(FP8X4), scales=op[2][:], in_=op[0][:])
+        def quantize(op, lo, hi):
+            nc.vector.quantize_mx(
+                out=op[1][:, lo:hi].bitcast(FP8X4), scales=op[2][:, lo:hi], in_=op[0][:, PACK * lo : PACK * hi]
+            )
 
         def product(bank, w, v, g):
             rows = slice(ROWS * g, ROWS * (g + 1))
@@ -85,12 +87,12 @@ def tile_rows_tnrowsoft_kernel(tc, x, w1, w2, tp, dx, og, base, out):
         nc.vector.memset(zero[:], 0.0)
 
         w1_raw = load("w1", w1, M)
-        x_raw = load("x", x, N)
         for r, vec in enumerate((tp, og)):
             nc.sync.dma_start(
                 out=rows_in[r:P:32, :].rearrange("q (g j) -> q g j", g=G),
                 in_=vec.rearrange("g (q j) o -> q g (j o)", j=32),
             )
+        x_raw = load("x", x, N)
         w2_raw = load("w2", w2, M)
         dx_raw = load("dx", dx, N)
         base_sb = sb.tile([P, G * N], F32, name="base_sb")
@@ -111,19 +113,9 @@ def tile_rows_tnrowsoft_kernel(tc, x, w1, w2, tp, dx, og, base, out):
         fac = sb.tile([P, 2 * G], F32, name="fac")
         neg_s, prob, z2s, part, dsum, scaled, res = (big(n) for n in ("neg_s", "prob", "z2s", "part", "dsum", "scaled", "res"))
 
-        inter_vector(w1_raw, w1q, 0, M)
-        quantize(w1q)
-
-        inter_vector(x_raw, xq, 0, X_SPLIT)
-        inter_scalar(x_raw, xq, X_SPLIT, N)
-        quantize(xq)
-        for g in range(G):
-            product(bank_a[g], w1q, xq, g)
-        inter_scalar(w2_raw, w2q, 0, M)
+        inter_vector(w1_raw, w1q, 0, 0, M)
         nc.vector.transpose(out=cols[:], in_=rows_in[:])
-        quantize(w2q)
-        for g in range(G):
-            product(bank_b[g], w2q, xq, g)
+        quantize(w1q, 0, M)
         tp_cols = cols[:, 0:P:32]
         og_cols = cols[:, 1:P:32]
         nc.vector.tensor_scalar(out=neg_tp[:], in0=tp_cols, scalar1=-1.0, scalar2=None, op0=ALU.mult)
@@ -132,8 +124,17 @@ def tile_rows_tnrowsoft_kernel(tc, x, w1, w2, tp, dx, og, base, out):
             out=gain[:, 1 : 2 * G : 2], in0=og_cols, scalar=float(N), in1=tp_cols, op0=ALU.mult, op1=ALU.mult
         )
 
+        inter_vector(x_raw, xq, 0, 0, X_SPLIT)
+        inter_scalar(x_raw, xq, 0, X_SPLIT, N)
+        quantize(xq, 0, N)
+        for g in range(G):
+            product(bank_a[g], w1q, xq, g)
+        inter_scalar(w2_raw, w2q, 0, 0, M)
+        quantize(w2q, 0, M)
+        product(bank_b[0], w2q, xq, 0)
+        product(bank_b[1], w2q, xq, 1)
         inter_gpsimd(dx_raw, dxq, 0, DX_SPLIT)
-        inter_scalar(dx_raw, dxq, DX_SPLIT, N)
+        inter_scalar(dx_raw, dxq, 0, DX_SPLIT, N)
 
         def row_max(g):
             nc.vector.tensor_scalar(
@@ -157,7 +158,6 @@ def tile_rows_tnrowsoft_kernel(tc, x, w1, w2, tp, dx, og, base, out):
 
         def scale_z2(g):
             nc.scalar.activation(out=z2s[g][:], in_=bank_b[g][:], func=ACT.Copy, scale=fac[:, 2 * g + 1 : 2 * g + 2])
-            product(bank_b[g], w2q, dxq, g)
 
         def mean_tz1(g):
             nc.vector.scalar_tensor_tensor(
@@ -184,22 +184,24 @@ def tile_rows_tnrowsoft_kernel(tc, x, w1, w2, tp, dx, og, base, out):
             eng.tensor_tensor(out=res[g][:], in0=scaled[g][:], in1=base_sb[:, g * N : (g + 1) * N], op=ALU.add)
             nc.sync.dma_start(out=out[g], in_=res[g][:])
 
-        row_max(0)
-        exp(0)
-        row_max(1)
-        exp(1)
-        row_max(2)
-        exp(2)
-        quantize(dxq)
         for g in range(3):
-            product(bank_a[g], w1q, dxq, g)
-        recip(0)
+            row_max(g)
+            exp(g)
+        quantize(dxq, 0, N)
+        product(bank_a[0], w1q, dxq, 0)
+        product(bank_a[1], w1q, dxq, 1)
         row_max(3)
-        product(bank_a[3], w1q, dxq, 3)
+        recip(0)
         factors(0)
         factors(1)
+        product(bank_b[2], w2q, xq, 2)
+        product(bank_b[3], w2q, xq, 3)
         scale_z2(0)
+        product(bank_b[0], w2q, dxq, 0)
         scale_z2(1)
+        product(bank_b[1], w2q, dxq, 1)
+        product(bank_a[2], w1q, dxq, 2)
+        product(bank_a[3], w1q, dxq, 3)
         exp(3)
         mean_tz1(0)
         mean_tz1(1)
@@ -208,7 +210,9 @@ def tile_rows_tnrowsoft_kernel(tc, x, w1, w2, tp, dx, og, base, out):
         factors(2)
         factors(3)
         scale_z2(2)
+        product(bank_b[2], w2q, dxq, 2)
         scale_z2(3)
+        product(bank_b[3], w2q, dxq, 3)
         add_tz2(0)
         weigh(nc.gpsimd, 0)
         finish(nc.gpsimd, 0)
@@ -216,12 +220,12 @@ def tile_rows_tnrowsoft_kernel(tc, x, w1, w2, tp, dx, og, base, out):
         mean_tz1(2)
         add_tz2(1)
         weigh(nc.gpsimd, 1)
-        finish(nc.gpsimd, 1)
         mean_tz1(3)
         centred(2)
         centred(3)
         add_tz2(2)
         add_tz2(3)
+        finish(nc.vector, 1)
         weigh(nc.vector, 2)
         weigh(nc.vector, 3)
         finish(nc.vector, 2)

@@ -16,8 +16,11 @@ ACT = mybir.ActivationFunctionType
 P = 128
 PACK = 4
 ROWS = D // PACK
-X_SPLIT = 336
-DX_SPLIT = 240
+RUN = 4
+BLOCK = 32
+HALF = N // 2
+X_VECTOR = 336
+DX_GPSIMD = 224
 
 
 def tile_rows_tnrowsoft_kernel(tc, x, w1, w2, tp, dx, og, base, out):
@@ -32,201 +35,224 @@ def tile_rows_tnrowsoft_kernel(tc, x, w1, w2, tp, dx, og, base, out):
             nc.sync.dma_start(out=raw[:], in_=src.rearrange("g (p j) n -> (g p) (j n)", j=PACK))
             return raw
 
-        def mx_tiles(name, width):
-            words = sb.tile([P, PACK * width], BF16, name=name + "_bf", align_bytes=64)
+        def mx_operand(name, width):
+            values = sb.tile([P, PACK * width], BF16, name=name + "_values", align_bytes=64)
             codes = sb.tile([P, width], U32, name=name + "_codes", align_bytes=64)
             scales = sb.tile([P, width], U8, name=name + "_scales", align_bytes=64)
-            return words, codes, scales
+            return values, codes, scales
 
-        def views(raw, words, at, lo, hi):
-            src = raw[:].rearrange("p (j c i) -> p c j i", j=PACK, i=4)[:, lo // 4 : hi // 4, :, :]
-            dst = words[:].rearrange("p (c i j) -> p c j i", i=4, j=PACK)[:, (at + lo) // 4 : (at + hi) // 4, :, :]
-            return src, dst
-
-        def inter_vector(raw, op, at, lo, hi):
-            src, dst = views(raw, op[0], at, lo, hi)
-            nc.vector.tensor_copy(out=dst, in_=src)
-
-        def inter_scalar(raw, op, at, lo, hi):
-            src, dst = views(raw, op[0], at, lo, hi)
-            nc.scalar.copy(out=dst, in_=src)
-
-        def inter_gpsimd(raw, op, lo, hi):
-            src = raw[:].rearrange("p (j n) -> p n j", j=PACK)[:, lo:hi, :]
-            dst = op[0][:].rearrange("p (n j) -> p n j", j=PACK)[:, lo:hi, :]
-            nc.gpsimd.tensor_scalar(out=dst, in0=src, scalar1=1.0, scalar2=0.0, op0=ALU.mult, op1=ALU.add)
-
-        def quantize(op, lo, hi):
-            nc.vector.quantize_mx(
-                out=op[1][:, lo:hi].bitcast(FP8X4), scales=op[2][:, lo:hi], in_=op[0][:, PACK * lo : PACK * hi]
+        def interleave(copy, raw, operand, lo, hi):
+            runs = slice(lo // RUN, hi // RUN)
+            copy(
+                out=operand[0][:].rearrange("p (c i j) -> p c j i", i=RUN, j=PACK)[:, runs, :, :],
+                in_=raw[:].rearrange("p (j c i) -> p c j i", j=PACK, i=RUN)[:, runs, :, :],
             )
 
-        def product(bank, w, v, g):
+        def interleave_gpsimd(raw, operand, lo, hi):
+            nc.gpsimd.tensor_scalar(
+                out=operand[0][:].rearrange("p (n j) -> p n j", j=PACK)[:, lo:hi, :],
+                in0=raw[:].rearrange("p (j n) -> p n j", j=PACK)[:, lo:hi, :],
+                scalar1=1.0,
+                scalar2=0.0,
+                op0=ALU.mult,
+                op1=ALU.add,
+            )
+
+        def quantize(operand, lo, hi):
+            values, codes, scales = operand
+            nc.vector.quantize_mx(
+                out=codes[:, lo:hi].bitcast(FP8X4), scales=scales[:, lo:hi], in_=values[:, PACK * lo : PACK * hi]
+            )
+
+        def product(banks, weights, moving, g):
             rows = slice(ROWS * g, ROWS * (g + 1))
             nc.tensor.matmul_mx(
-                out=bank[:],
-                lhsT=w[1][rows, :].bitcast(FP8X4),
-                lhsT_scale=w[2][rows, :],
-                rhs=v[1][rows, :].bitcast(FP8X4),
-                rhs_scale=v[2][rows, :],
+                out=banks[g][:],
+                lhsT=weights[1][rows, :].bitcast(FP8X4),
+                lhsT_scale=weights[2][rows, :],
+                rhs=moving[1][rows, :].bitcast(FP8X4),
+                rhs_scale=moving[2][rows, :],
                 start=True,
                 stop=True,
             )
 
-        def big(name):
+        def per_group(name):
             return [sb.tile([P, N], F32, name=name + str(g)) for g in range(G)]
 
-        bank_a = [ps.tile([P, N], F32, name="bank_a" + str(g)) for g in range(G)]
-        bank_b = [ps.tile([P, N], F32, name="bank_b" + str(g)) for g in range(G)]
+        w1_banks = [ps.tile([P, N], F32, name="w1_bank" + str(g)) for g in range(G)]
+        w2_banks = [ps.tile([P, N], F32, name="w2_bank" + str(g)) for g in range(G)]
 
-        rows_in = sb.tile([P, P], F32, name="rows_in", align_bytes=64)
-        cols = sb.tile([P, P], F32, name="cols", align_bytes=64)
-        warm = sb.tile([P, 1], F32, name="warm")
-        zero = sb.tile([P, 1], F32, name="zero")
-        nc.vector.memset(rows_in[:], 0.0)
-        nc.vector.memset(zero[:], 0.0)
+        vec_rows = sb.tile([P, G * BLOCK], F32, name="vec_rows", align_bytes=64)
+        vec_cols = sb.tile([P, G * BLOCK], F32, name="vec_cols", align_bytes=64)
+        nc.vector.memset(vec_rows[:], 0.0)
 
         w1_raw = load("w1", w1, M)
-        for r, vec in enumerate((tp, og)):
+        for place, vec in enumerate((tp, og)):
             nc.sync.dma_start(
-                out=rows_in[r:P:32, :].rearrange("q (g j) -> q g j", g=G),
-                in_=vec.rearrange("g (q j) o -> q g (j o)", j=32),
+                out=vec_rows[place:P:BLOCK, :].rearrange("q (g i) -> q g i", g=G),
+                in_=vec.rearrange("g (q i) o -> q g (i o)", i=BLOCK),
             )
         x_raw = load("x", x, N)
         w2_raw = load("w2", w2, M)
         dx_raw = load("dx", dx, N)
         base_sb = sb.tile([P, G * N], F32, name="base_sb")
         nc.sync.dma_start(out=base_sb[:].rearrange("m (g n) -> m g n", g=G), in_=base.rearrange("g m n -> m g n"))
-        nc.scalar.activation(out=warm[:], in_=zero[:], func=ACT.Exp)
 
-        w1q = mx_tiles("w1", M)
-        w2q = mx_tiles("w2", M)
-        xq = mx_tiles("x", N)
-        dxq = mx_tiles("dx", N)
+        w1_mx = mx_operand("w1", M)
+        w2_mx = mx_operand("w2", M)
+        x_mx = mx_operand("x", N)
+        dx_mx = mx_operand("dx", N)
 
         neg_tp = sb.tile([P, G], F32, name="neg_tp")
-        gain = sb.tile([P, 2 * G], F32, name="gain")
+        gains = sb.tile([P, 2 * G], F32, name="gains")
         neg_max = sb.tile([P, G], F32, name="neg_max")
-        zsum = sb.tile([P, G], F32, name="zsum")
+        prob_sum = sb.tile([P, G], F32, name="prob_sum")
         inv = sb.tile([P, G], F32, name="inv")
         mean = sb.tile([P, G], F32, name="mean")
-        fac = sb.tile([P, 2 * G], F32, name="fac")
-        neg_s, prob, z2s, part, dsum, scaled, res = (big(n) for n in ("neg_s", "prob", "z2s", "part", "dsum", "scaled", "res"))
-
-        inter_vector(w1_raw, w1q, 0, 0, M)
-        nc.vector.transpose(out=cols[:], in_=rows_in[:])
-        quantize(w1q, 0, M)
-        tp_cols = cols[:, 0:P:32]
-        og_cols = cols[:, 1:P:32]
-        nc.vector.tensor_scalar(out=neg_tp[:], in0=tp_cols, scalar1=-1.0, scalar2=None, op0=ALU.mult)
-        nc.vector.tensor_scalar(out=gain[:, 0 : 2 * G : 2], in0=og_cols, scalar1=float(N), scalar2=None, op0=ALU.mult)
-        nc.vector.scalar_tensor_tensor(
-            out=gain[:, 1 : 2 * G : 2], in0=og_cols, scalar=float(N), in1=tp_cols, op0=ALU.mult, op1=ALU.mult
+        factors = sb.tile([P, 2 * G], F32, name="factors")
+        neg_score, prob, z2_scaled, centred, inner, weighed, result = (
+            per_group(name) for name in ("neg_score", "prob", "z2_scaled", "centred", "inner", "weighed", "result")
         )
-
-        inter_vector(x_raw, xq, 0, 0, X_SPLIT)
-        inter_scalar(x_raw, xq, 0, X_SPLIT, N)
-        quantize(xq, 0, N)
-        for g in range(G):
-            product(bank_a[g], w1q, xq, g)
-        inter_scalar(w2_raw, w2q, 0, 0, M)
-        quantize(w2q, 0, M)
-        product(bank_b[0], w2q, xq, 0)
-        product(bank_b[1], w2q, xq, 1)
-        inter_gpsimd(dx_raw, dxq, 0, DX_SPLIT)
-        inter_scalar(dx_raw, dxq, 0, DX_SPLIT, N)
 
         def row_max(g):
             nc.vector.tensor_scalar(
-                out=neg_s[g][:], in0=bank_a[g][:], scalar1=neg_tp[:, g : g + 1], scalar2=None,
-                op0=ALU.mult, op1=ALU.min, accum_out=neg_max[:, g : g + 1],
+                out=neg_score[g][:],
+                in0=w1_banks[g][:],
+                scalar1=neg_tp[:, g : g + 1],
+                scalar2=None,
+                op0=ALU.mult,
+                op1=ALU.min,
+                accum_out=neg_max[:, g : g + 1],
             )
 
-        def exp(g):
+        def exponential(g):
             nc.scalar.activation(
-                out=prob[g][:], in_=neg_s[g][:], func=ACT.Exp, scale=-1.0,
-                bias=neg_max[:, g : g + 1], accum_out=zsum[:, g : g + 1],
+                out=prob[g][:],
+                in_=neg_score[g][:],
+                func=ACT.Exp,
+                scale=-1.0,
+                bias=neg_max[:, g : g + 1],
+                accum_out=prob_sum[:, g : g + 1],
             )
 
-        def recip(g0):
-            nc.vector.reciprocal(out=inv[:, g0 : g0 + 2], in_=zsum[:, g0 : g0 + 2])
+        def invert_sums(pair):
+            cols = slice(pair[0], pair[1] + 1)
+            nc.vector.reciprocal(out=inv[:, cols], in_=prob_sum[:, cols])
 
-        def factors(g):
+        def make_factors(g):
+            cols = slice(2 * g, 2 * g + 2)
+            nc.scalar.activation(out=factors[:, cols], in_=gains[:, cols], func=ACT.Copy, scale=inv[:, g : g + 1])
+
+        def swap_z2_for_tz2(g):
             nc.scalar.activation(
-                out=fac[:, 2 * g : 2 * g + 2], in_=gain[:, 2 * g : 2 * g + 2], func=ACT.Copy, scale=inv[:, g : g + 1]
+                out=z2_scaled[g][:], in_=w2_banks[g][:], func=ACT.Copy, scale=factors[:, 2 * g + 1 : 2 * g + 2]
+            )
+            product(w2_banks, w2_mx, dx_mx, g)
+
+        def row_mean(g):
+            nc.vector.scalar_tensor_tensor(
+                out=centred[g][:],
+                in0=w1_banks[g][:],
+                scalar=inv[:, g : g + 1],
+                in1=prob[g][:],
+                op0=ALU.mult,
+                op1=ALU.mult,
+                accum_out=mean[:, g : g + 1],
             )
 
-        def scale_z2(g):
-            nc.scalar.activation(out=z2s[g][:], in_=bank_b[g][:], func=ACT.Copy, scale=fac[:, 2 * g + 1 : 2 * g + 2])
-
-        def mean_tz1(g):
+        def centre(g):
             nc.vector.scalar_tensor_tensor(
-                out=part[g][:], in0=bank_a[g][:], scalar=inv[:, g : g + 1], in1=prob[g][:],
-                op0=ALU.mult, op1=ALU.mult, accum_out=mean[:, g : g + 1],
-            )
-
-        def centred(g):
-            nc.vector.scalar_tensor_tensor(
-                out=part[g][:], in0=bank_a[g][:], scalar=mean[:, g : g + 1], in1=z2s[g][:],
-                op0=ALU.subtract, op1=ALU.mult,
+                out=centred[g][:],
+                in0=w1_banks[g][:],
+                scalar=mean[:, g : g + 1],
+                in1=z2_scaled[g][:],
+                op0=ALU.subtract,
+                op1=ALU.mult,
             )
 
         def add_tz2(g):
             nc.vector.scalar_tensor_tensor(
-                out=dsum[g][:], in0=bank_b[g][:], scalar=fac[:, 2 * g : 2 * g + 1], in1=part[g][:],
-                op0=ALU.mult, op1=ALU.add,
+                out=inner[g][:],
+                in0=w2_banks[g][:],
+                scalar=factors[:, 2 * g : 2 * g + 1],
+                in1=centred[g][:],
+                op0=ALU.mult,
+                op1=ALU.add,
             )
 
-        def weigh(eng, g):
-            eng.tensor_tensor(out=scaled[g][:], in0=dsum[g][:], in1=prob[g][:], op=ALU.mult)
+        def weigh(engine, g):
+            engine.tensor_tensor(out=weighed[g][:], in0=inner[g][:], in1=prob[g][:], op=ALU.mult)
 
-        def finish(eng, g):
-            eng.tensor_tensor(out=res[g][:], in0=scaled[g][:], in1=base_sb[:, g * N : (g + 1) * N], op=ALU.add)
-            nc.sync.dma_start(out=out[g], in_=res[g][:])
+        def add_base_and_store(engine, g):
+            engine.tensor_tensor(out=result[g][:], in0=weighed[g][:], in1=base_sb[:, g * N : (g + 1) * N], op=ALU.add)
+            nc.sync.dma_start(out=out[g], in_=result[g][:])
 
-        for g in range(3):
+        interleave(nc.vector.tensor_copy, w1_raw, w1_mx, 0, M)
+        nc.vector.transpose(out=vec_cols[:], in_=vec_rows[:])
+        quantize(w1_mx, 0, M)
+        tp_cols = vec_cols[:, 0 : G * BLOCK : BLOCK]
+        og_cols = vec_cols[:, 1 : G * BLOCK : BLOCK]
+        nc.vector.tensor_scalar(out=neg_tp[:], in0=tp_cols, scalar1=-1.0, scalar2=None, op0=ALU.mult)
+        nc.vector.tensor_scalar(out=gains[:, 0 : 2 * G : 2], in0=og_cols, scalar1=float(N), scalar2=None, op0=ALU.mult)
+        nc.vector.scalar_tensor_tensor(
+            out=gains[:, 1 : 2 * G : 2], in0=og_cols, scalar=float(N), in1=tp_cols, op0=ALU.mult, op1=ALU.mult
+        )
+
+        interleave(nc.vector.tensor_copy, x_raw, x_mx, 0, HALF)
+        interleave(nc.vector.tensor_copy, x_raw, x_mx, HALF, X_VECTOR)
+        interleave(nc.scalar.copy, x_raw, x_mx, X_VECTOR, N)
+        quantize(x_mx, 0, HALF)
+        quantize(x_mx, HALF, N)
+        for g in range(G):
+            product(w1_banks, w1_mx, x_mx, g)
+        interleave(nc.scalar.copy, w2_raw, w2_mx, 0, M)
+        quantize(w2_mx, 0, M)
+
+        first, second = (0, 1), (2, 3)
+        for g in first:
+            product(w2_banks, w2_mx, x_mx, g)
+        interleave_gpsimd(dx_raw, dx_mx, 0, DX_GPSIMD)
+        interleave(nc.scalar.copy, dx_raw, dx_mx, DX_GPSIMD, N)
+
+        for g in range(G - 1):
             row_max(g)
-            exp(g)
-        quantize(dxq, 0, N)
-        product(bank_a[0], w1q, dxq, 0)
-        product(bank_a[1], w1q, dxq, 1)
-        row_max(3)
-        recip(0)
-        factors(0)
-        factors(1)
-        product(bank_b[2], w2q, xq, 2)
-        product(bank_b[3], w2q, xq, 3)
-        scale_z2(0)
-        product(bank_b[0], w2q, dxq, 0)
-        scale_z2(1)
-        product(bank_b[1], w2q, dxq, 1)
-        product(bank_a[2], w1q, dxq, 2)
-        product(bank_a[3], w1q, dxq, 3)
-        exp(3)
-        mean_tz1(0)
-        mean_tz1(1)
-        centred(0)
-        recip(2)
-        factors(2)
-        factors(3)
-        scale_z2(2)
-        product(bank_b[2], w2q, dxq, 2)
-        scale_z2(3)
-        product(bank_b[3], w2q, dxq, 3)
+            exponential(g)
+        quantize(dx_mx, 0, N)
+        for g in first:
+            product(w1_banks, w1_mx, dx_mx, g)
+        row_max(G - 1)
+        invert_sums(first)
+        for g in first:
+            make_factors(g)
+        product(w2_banks, w2_mx, x_mx, second[0])
+        for g in first:
+            swap_z2_for_tz2(g)
+        product(w1_banks, w1_mx, dx_mx, second[0])
+        product(w2_banks, w2_mx, x_mx, second[1])
+        product(w1_banks, w1_mx, dx_mx, second[1])
+        exponential(G - 1)
+
+        for g in first:
+            row_mean(g)
+        centre(0)
+        invert_sums(second)
+        for g in second:
+            make_factors(g)
+        for g in second:
+            swap_z2_for_tz2(g)
         add_tz2(0)
+
         weigh(nc.gpsimd, 0)
-        finish(nc.gpsimd, 0)
-        centred(1)
-        mean_tz1(2)
+        add_base_and_store(nc.gpsimd, 0)
+        centre(1)
+        row_mean(2)
         add_tz2(1)
         weigh(nc.gpsimd, 1)
-        mean_tz1(3)
-        centred(2)
-        centred(3)
-        add_tz2(2)
-        add_tz2(3)
-        finish(nc.vector, 1)
-        weigh(nc.vector, 2)
-        weigh(nc.vector, 3)
-        finish(nc.vector, 2)
-        finish(nc.vector, 3)
+        row_mean(3)
+        for step in (centre, add_tz2):
+            for g in second:
+                step(g)
+        add_base_and_store(nc.vector, 1)
+        for step in (weigh, add_base_and_store):
+            for g in second:
+                step(nc.vector, g)

from contextlib import ExitStack

import concourse.mybir as mybir

G, D, M, N = 4, 128, 128, 512
FLOPS = 4 * 2 * G * D * M * N

F32 = mybir.dt.float32
BF16 = mybir.dt.bfloat16
U32 = mybir.dt.uint32
U8 = mybir.dt.uint8
FP8X4 = mybir.dt.float8_e4m3fn_x4
ALU = mybir.AluOpType
ACT = mybir.ActivationFunctionType

P = 128
PACK = 4
ROWS = D // PACK
RUN = 4
BLOCK = 32
HALF = N // 2
X_VECTOR = 336
DX_GPSIMD = 224


def tile_rows_tnrowsoft_kernel(tc, x, w1, w2, tp, dx, og, base, out):
    nc = tc.nc
    with ExitStack() as ctx:
        sb = ctx.enter_context(tc.tile_pool(name="sb", bufs=1))
        ps = ctx.enter_context(tc.psum_pool(name="ps", bufs=1))
        ctx.enter_context(tc.manual_schedule())

        def load(name, src, width):
            raw = sb.tile([P, PACK * width], F32, name=name + "_raw", align_bytes=64)
            nc.sync.dma_start(out=raw[:], in_=src.rearrange("g (p j) n -> (g p) (j n)", j=PACK))
            return raw

        def mx_operand(name, width):
            values = sb.tile([P, PACK * width], BF16, name=name + "_values", align_bytes=64)
            codes = sb.tile([P, width], U32, name=name + "_codes", align_bytes=64)
            scales = sb.tile([P, width], U8, name=name + "_scales", align_bytes=64)
            return values, codes, scales

        def interleave(copy, raw, operand, lo, hi):
            runs = slice(lo // RUN, hi // RUN)
            copy(
                out=operand[0][:].rearrange("p (c i j) -> p c j i", i=RUN, j=PACK)[:, runs, :, :],
                in_=raw[:].rearrange("p (j c i) -> p c j i", j=PACK, i=RUN)[:, runs, :, :],
            )

        def interleave_gpsimd(raw, operand, lo, hi):
            nc.gpsimd.tensor_scalar(
                out=operand[0][:].rearrange("p (n j) -> p n j", j=PACK)[:, lo:hi, :],
                in0=raw[:].rearrange("p (j n) -> p n j", j=PACK)[:, lo:hi, :],
                scalar1=1.0,
                scalar2=0.0,
                op0=ALU.mult,
                op1=ALU.add,
            )

        def quantize(operand, lo, hi):
            values, codes, scales = operand
            nc.vector.quantize_mx(
                out=codes[:, lo:hi].bitcast(FP8X4), scales=scales[:, lo:hi], in_=values[:, PACK * lo : PACK * hi]
            )

        def product(banks, weights, moving, g):
            rows = slice(ROWS * g, ROWS * (g + 1))
            nc.tensor.matmul_mx(
                out=banks[g][:],
                lhsT=weights[1][rows, :].bitcast(FP8X4),
                lhsT_scale=weights[2][rows, :],
                rhs=moving[1][rows, :].bitcast(FP8X4),
                rhs_scale=moving[2][rows, :],
                start=True,
                stop=True,
            )

        def per_group(name):
            return [sb.tile([P, N], F32, name=name + str(g)) for g in range(G)]

        w1_banks = [ps.tile([P, N], F32, name="w1_bank" + str(g)) for g in range(G)]
        w2_banks = [ps.tile([P, N], F32, name="w2_bank" + str(g)) for g in range(G)]

        vec_rows = sb.tile([P, G * BLOCK], F32, name="vec_rows", align_bytes=64)
        vec_cols = sb.tile([P, G * BLOCK], F32, name="vec_cols", align_bytes=64)
        nc.vector.memset(vec_rows[:], 0.0)

        w1_raw = load("w1", w1, M)
        for place, vec in enumerate((tp, og)):
            nc.sync.dma_start(
                out=vec_rows[place:P:BLOCK, :].rearrange("q (g i) -> q g i", g=G),
                in_=vec.rearrange("g (q i) o -> q g (i o)", i=BLOCK),
            )
        x_raw = load("x", x, N)
        w2_raw = load("w2", w2, M)
        dx_raw = load("dx", dx, N)
        base_sb = sb.tile([P, G * N], F32, name="base_sb")
        nc.sync.dma_start(out=base_sb[:].rearrange("m (g n) -> m g n", g=G), in_=base.rearrange("g m n -> m g n"))

        w1_mx = mx_operand("w1", M)
        w2_mx = mx_operand("w2", M)
        x_mx = mx_operand("x", N)
        dx_mx = mx_operand("dx", N)

        neg_tp = sb.tile([P, G], F32, name="neg_tp")
        gains = sb.tile([P, 2 * G], F32, name="gains")
        neg_max = sb.tile([P, G], F32, name="neg_max")
        prob_sum = sb.tile([P, G], F32, name="prob_sum")
        inv = sb.tile([P, G], F32, name="inv")
        mean = sb.tile([P, G], F32, name="mean")
        factors = sb.tile([P, 2 * G], F32, name="factors")
        neg_score, prob, z2_scaled, centred, inner, weighed, result = (
            per_group(name) for name in ("neg_score", "prob", "z2_scaled", "centred", "inner", "weighed", "result")
        )

        def row_max(g):
            nc.vector.tensor_scalar(
                out=neg_score[g][:],
                in0=w1_banks[g][:],
                scalar1=neg_tp[:, g : g + 1],
                scalar2=None,
                op0=ALU.mult,
                op1=ALU.min,
                accum_out=neg_max[:, g : g + 1],
            )

        def exponential(g):
            nc.scalar.activation(
                out=prob[g][:],
                in_=neg_score[g][:],
                func=ACT.Exp,
                scale=-1.0,
                bias=neg_max[:, g : g + 1],
                accum_out=prob_sum[:, g : g + 1],
            )

        def invert_sums(pair):
            cols = slice(pair[0], pair[1] + 1)
            nc.vector.reciprocal(out=inv[:, cols], in_=prob_sum[:, cols])

        def make_factors(g):
            cols = slice(2 * g, 2 * g + 2)
            nc.scalar.activation(out=factors[:, cols], in_=gains[:, cols], func=ACT.Copy, scale=inv[:, g : g + 1])

        def swap_z2_for_tz2(g):
            nc.scalar.activation(
                out=z2_scaled[g][:], in_=w2_banks[g][:], func=ACT.Copy, scale=factors[:, 2 * g + 1 : 2 * g + 2]
            )
            product(w2_banks, w2_mx, dx_mx, g)

        def row_mean(g):
            nc.vector.scalar_tensor_tensor(
                out=centred[g][:],
                in0=w1_banks[g][:],
                scalar=inv[:, g : g + 1],
                in1=prob[g][:],
                op0=ALU.mult,
                op1=ALU.mult,
                accum_out=mean[:, g : g + 1],
            )

        def centre(g):
            nc.vector.scalar_tensor_tensor(
                out=centred[g][:],
                in0=w1_banks[g][:],
                scalar=mean[:, g : g + 1],
                in1=z2_scaled[g][:],
                op0=ALU.subtract,
                op1=ALU.mult,
            )

        def add_tz2(g):
            nc.vector.scalar_tensor_tensor(
                out=inner[g][:],
                in0=w2_banks[g][:],
                scalar=factors[:, 2 * g : 2 * g + 1],
                in1=centred[g][:],
                op0=ALU.mult,
                op1=ALU.add,
            )

        def weigh(engine, g):
            engine.tensor_tensor(out=weighed[g][:], in0=inner[g][:], in1=prob[g][:], op=ALU.mult)

        def add_base_and_store(engine, g):
            engine.tensor_tensor(out=result[g][:], in0=weighed[g][:], in1=base_sb[:, g * N : (g + 1) * N], op=ALU.add)
            nc.sync.dma_start(out=out[g], in_=result[g][:])

        interleave(nc.vector.tensor_copy, w1_raw, w1_mx, 0, M)
        nc.vector.transpose(out=vec_cols[:], in_=vec_rows[:])
        quantize(w1_mx, 0, M)
        tp_cols = vec_cols[:, 0 : G * BLOCK : BLOCK]
        og_cols = vec_cols[:, 1 : G * BLOCK : BLOCK]
        nc.vector.tensor_scalar(out=neg_tp[:], in0=tp_cols, scalar1=-1.0, scalar2=None, op0=ALU.mult)
        nc.vector.tensor_scalar(out=gains[:, 0 : 2 * G : 2], in0=og_cols, scalar1=float(N), scalar2=None, op0=ALU.mult)
        nc.vector.scalar_tensor_tensor(
            out=gains[:, 1 : 2 * G : 2], in0=og_cols, scalar=float(N), in1=tp_cols, op0=ALU.mult, op1=ALU.mult
        )

        interleave(nc.vector.tensor_copy, x_raw, x_mx, 0, HALF)
        interleave(nc.vector.tensor_copy, x_raw, x_mx, HALF, X_VECTOR)
        interleave(nc.scalar.copy, x_raw, x_mx, X_VECTOR, N)
        quantize(x_mx, 0, HALF)
        quantize(x_mx, HALF, N)
        for g in range(G):
            product(w1_banks, w1_mx, x_mx, g)
        interleave(nc.scalar.copy, w2_raw, w2_mx, 0, M)
        quantize(w2_mx, 0, M)

        first, second = (0, 1), (2, 3)
        for g in first:
            product(w2_banks, w2_mx, x_mx, g)
        interleave_gpsimd(dx_raw, dx_mx, 0, DX_GPSIMD)
        interleave(nc.scalar.copy, dx_raw, dx_mx, DX_GPSIMD, N)

        for g in range(G - 1):
            row_max(g)
            exponential(g)
        quantize(dx_mx, 0, N)
        for g in first:
            product(w1_banks, w1_mx, dx_mx, g)
        row_max(G - 1)
        invert_sums(first)
        for g in first:
            make_factors(g)
        product(w2_banks, w2_mx, x_mx, second[0])
        for g in first:
            swap_z2_for_tz2(g)
        product(w1_banks, w1_mx, dx_mx, second[0])
        product(w2_banks, w2_mx, x_mx, second[1])
        product(w1_banks, w1_mx, dx_mx, second[1])
        exponential(G - 1)

        for g in first:
            row_mean(g)
        centre(0)
        invert_sums(second)
        for g in second:
            make_factors(g)
        for g in second:
            swap_z2_for_tz2(g)
        add_tz2(0)

        weigh(nc.gpsimd, 0)
        add_base_and_store(nc.gpsimd, 0)
        centre(1)
        row_mean(2)
        add_tz2(1)
        weigh(nc.gpsimd, 1)
        row_mean(3)
        for step in (centre, add_tz2):
            for g in second:
                step(g)
        add_base_and_store(nc.vector, 1)
        for step in (weigh, add_base_and_store):
            for g in second:
                step(nc.vector, g)
